import numpy as np
import ml_dtypes


def mxq(x, axis, fmt="e4m3"):
    dtype, down = {"e4m3": (ml_dtypes.float8_e4m3fn, 7), "e5m2": (ml_dtypes.float8_e5m2, 14)}[fmt]
    v = np.moveaxis(np.asarray(x, np.float32).astype(ml_dtypes.bfloat16).astype(np.float64), axis, -1)
    blocks = v.reshape(v.shape[:-1] + (-1, 32))
    amax = np.abs(blocks).max(-1, keepdims=True)
    byte = np.maximum(np.where(amax > 0, np.frexp(amax)[1] - 1 + 127, 0) - down, 1)
    scale = np.exp2(byte - 127.0)
    codes = (blocks / scale).astype(np.float32).astype(dtype).astype(np.float64)
    return np.moveaxis((codes * scale).reshape(v.shape), -1, axis)


WIDE = False


def mx_kscale(k):
    if not WIDE:
        return np.ones(k)
    levels = np.array([10, -10, 5, -5, 0])
    if k % 512:
        return np.exp2(np.random.permutation(np.resize(levels, k // 32))).repeat(32)
    a = np.empty((k // 512, 16))
    for p in range(k // 512):
        a[p, :8] = np.random.permutation(np.resize(levels, 8))
        for g in range(8):
            far = levels[np.abs(levels - a[p, g]) >= 10]
            a[p, g + 8] = far[np.random.randint(len(far))]
    return np.exp2(a.ravel()).repeat(32)


def f64(x):
    return np.asarray(x).astype(np.float64)


def striped(idx):
    return np.tile(idx.reshape(-1, 16).T, (8, 1)).astype(np.uint16)


def unstriped(offs):
    return offs[:16].T.reshape(-1).astype(np.int64)


E2M1 = np.array([0.0, 0.5, 1.0, 1.5, 2.0, 3.0, 4.0, 6.0, -0.0, -0.5, -1.0, -1.5, -2.0, -3.0, -4.0, -6.0])


def pack_weight(w, fmt):
    k, n = w.shape
    w = f64(np.asarray(w, np.float32).astype(ml_dtypes.bfloat16)).reshape(k // 32, 32, n)
    amax = np.abs(w).max(1)
    if fmt == "e4m3":
        byte = np.frexp(amax)[1] - 1 + 127 - 7
    else:
        mant, ex = np.frexp(amax / 6.0)
        byte = np.where(mant > 0.5, ex, ex - 1) + 127
    byte = np.clip(np.where(amax > 0, byte, 1), 1, 254)
    scaled = (w * np.exp2(127.0 - byte)[:, None, :]).reshape(k, n).astype(np.float32)
    by_word = np.ascontiguousarray(scaled.reshape(k // 512, 128, 4, n).transpose(0, 1, 3, 2))
    if fmt == "e4m3":
        words = by_word.astype(ml_dtypes.float8_e4m3fn).view(np.uint8)
    else:
        c = by_word.astype(ml_dtypes.float4_e2m1fn).view(np.uint8) & 0xF
        words = (c[..., 0::2] | (c[..., 1::2] << 4)).reshape(k // 512, 128, 2 * n)
    return np.ascontiguousarray(words), np.ascontiguousarray(byte.astype(np.uint8).reshape(k // 512, 16, n))


def unpack_weight(words, scales, fmt):
    g, _, n = scales.shape
    words = np.ascontiguousarray(words).reshape(g, 128, n, -1)
    if fmt == "e4m3":
        vals = words.view(ml_dtypes.float8_e4m3fn).astype(np.float64)
    else:
        nib = np.empty((g, 128, n, 4), np.uint8)
        nib[..., 0::2] = words & 0xF
        nib[..., 1::2] = words >> 4
        vals = E2M1[nib]
    vals = vals * np.repeat(np.exp2(scales.astype(np.float64) - 127.0), 8, axis=1)[..., None]
    return vals.transpose(0, 1, 3, 2).reshape(g * 512, n)


def gelu(v):
    return 0.5 * v * (1.0 + np.tanh(np.sqrt(2.0 / np.pi) * (v + 0.044715 * v**3)))


def striped8(idx):
    return np.concatenate([v.reshape(-1, 16).T for v in idx]).astype(np.uint16)


def unstriped8(offs):
    return np.stack([offs[16 * g:16 * g + 16].T.reshape(-1) for g in range(8)]).astype(np.int64)


def heads(h, wgt, idx8):
    r = np.arange(h.shape[0])
    return wgt[r // 4 % 128] * h[r[:, None], idx8[r % 512 // 64]]


def put_heads(h, wgs, idx8, t2):
    r = np.arange(h.shape[0])
    page = np.zeros((h.shape[0], t2))
    page[r[:, None], idx8[r % 512 // 64]] = wgs[r // 4 % 128] * h
    return page


K, H, N, T, S, P, T2 = 1024, 512, 384, 4096, 1024, 1024, 2048

def setup_inputs():
    n = np.random.standard_normal
    s = mx_kscale(K)[:, None]
    u = mx_kscale(H)[:, None]
    d = {}
    d["tab_words"], d["tab_scales"] = pack_weight(n((K, T)) * s, "e4m3")
    d["offs"] = striped(np.random.permutation(T)[:S])
    d["offs2"] = striped8(np.stack([np.random.permutation(T2)[:S] for _ in range(8)]))
    d["offs3"] = striped8(np.stack([np.random.permutation(T2)[:P] for _ in range(8)]))
    d["w1_words"], d["w1_scales"] = pack_weight(n((K, H)) / s / K**0.5, "e2m1")
    d["gain"] = (np.exp(0.4 * n(H)) * u[:, 0]).astype(np.float32)
    d["wgs"] = np.repeat(np.random.uniform(0.5, 2.0, (8, S)), 16, axis=0).astype(np.float32)
    d["wgt"] = np.repeat(np.random.uniform(0.5, 2.0, (8, P)), 16, axis=0).astype(np.float32)
    d["flex"] = (n((H, P)) * u).astype(np.float32)
    d["wa"] = (n((H, N)) / u / H**0.5).astype(np.float32)
    d["wb"] = (n((H, N)) / u / H**0.5).astype(np.float32)
    d["wc_words"], d["wc_scales"] = pack_weight(n((H, N)) / u / H**0.5, "e4m3")
    return d

def reference(tab_words, tab_scales, offs, offs2, offs3, w1_words, w1_scales, gain, wgs, wgt, flex, wa, wb, wc_words, wc_scales):
    v = unpack_weight(tab_words, tab_scales, "e4m3")[:, unstriped(offs)]
    w1 = unpack_weight(w1_words, w1_scales, "e2m1")
    h = f64(gain)[:, None] * (w1.T @ v)
    page = put_heads(h, f64(wgs), unstriped8(offs2), T2)
    x = heads(page, f64(wgt), unstriped8(offs3))
    z = mxq(x + f64(flex), 0, "e4m3")
    wc = unpack_weight(wc_words, wc_scales, "e4m3")
    ya = mxq(f64(wa), 0, "e4m3").T @ z
    yb = mxq(f64(wb), 0, "e4m3").T @ z
    yc = wc.T @ z
    return np.maximum(ya, yb) - np.abs(yc)

@@ -1,0 +1,239 @@
+from contextlib import ExitStack
+
+import concourse.mybir as mybir
+
+K, H, N, T, S, M, T2 = 1024, 512, 384, 4096, 1024, 1024, 2048
+FLOPS = 2 * K * H * S + 3 * 2 * H * N * M
+
+F32 = mybir.dt.float32
+BF16 = mybir.dt.bfloat16
+I32 = mybir.dt.int32
+U32 = mybir.dt.uint32
+U16 = mybir.dt.uint16
+U8 = mybir.dt.uint8
+FP8X4 = mybir.dt.float8_e4m3fn_x4
+FP4X4 = mybir.dt.float4_e2m1fn_x4
+ALU = mybir.AluOpType
+ACT = mybir.ActivationFunctionType
+
+P = 128
+PACK = 4
+PASSES = K // (P * PACK)
+BANK = 512
+HALVES = S // BANK
+NB = N // P
+SUB = 128
+CHUNKS = (256, 256, 256, 128, 128)
+
+
+def tile_list_brace_pad_scores_kernel(
+    tc, tab_words, tab_scales, offs, offs2, offs3, w1_words, w1_scales, gain, wgs, wgt, flex, wa, wb,
+    wc_words, wc_scales, out,
+):
+    nc = tc.nc
+    with ExitStack() as ctx:
+        lists = ctx.enter_context(tc.tile_pool(name="lists", bufs=1))
+        keep = ctx.enter_context(tc.tile_pool(name="keep", bufs=1))
+        ring = ctx.enter_context(tc.tile_pool(name="ring", bufs=2))
+        psum = ctx.enter_context(tc.psum_pool(name="psum", bufs=8))
+
+        def kept(shape, dtype, name, after=None):
+            return keep.tile(shape, dtype, name=name, tag=after or name, align_bytes=64)
+
+        tab_s = kept([P, T // 4], I32, "tab_s")
+        for q in range(4):
+            nc.vector.memset(tab_s[32 * q : 32 * q + 24, :], 0)
+        w1_s_raw = kept([P, PASSES, H], U8, "w1_s_raw")
+        nc.gpsimd.memset(w1_s_raw[:].rearrange("p a c -> p (a c)").bitcast(I32), 0)
+        v_s = [kept([P, S], U8, "v_s%d" % a) for a in range(PASSES)]
+        for a in range(PASSES):
+            nc.vector.memset(v_s[a][:].bitcast(I32), 0)
+
+        idx = lists.tile([P, S // 16], U16, name="idx")
+        idx2 = lists.tile([P, S // 16], U16, name="idx2")
+        idx3 = lists.tile([P, M // 16], U16, name="idx3")
+        nc.sync.dma_start(idx[:], offs)
+        for q in range(4):
+            nc.sync.dma_start(tab_s[32 * q + 24 : 32 * q + 32, :], tab_scales[:, 4 * q : 4 * q + 4, :].bitcast(I32))
+        w1_raw = kept([P, PASSES, 2 * H], U8, "w1_raw")
+        nc.sync.dma_start(w1_raw[:].bitcast(I32), w1_words.rearrange("a p c -> p a c").bitcast(I32))
+        tab_w = [kept([P, T], I32, "tab_w%d" % a) for a in range(PASSES)]
+        for a in range(PASSES):
+            nc.sync.dma_start(tab_w[a][:], tab_words[a].rearrange("p n t -> p (n t)").bitcast(I32))
+        for q in range(4):
+            nc.gpsimd.dma_start(
+                w1_s_raw[32 * q : 32 * q + 4, :, :].bitcast(I32),
+                w1_scales[:, 4 * q : 4 * q + 4, :].rearrange("a r c -> r a c").bitcast(I32),
+            )
+        nc.sync.dma_start(idx2[:], offs2)
+        nc.sync.dma_start(idx3[:], offs3)
+        gain_sb = kept([P, PACK], F32, "gain_sb")
+        nc.gpsimd.dma_start(gain_sb[:], gain.rearrange("(p t) -> p t", t=PACK))
+
+        pages = [kept([P, T2], F32, "page%d" % i) for i in range(2)]
+        nc.gpsimd.memset(pages[0][:], 0.0)
+
+        picked_s = kept([P, S], U8, "picked_s")
+        nc.vector.tensor_copy(picked_s[:], tab_s[:].bitcast(U8).indirect(idx[:]))
+        for a in range(PASSES):
+            nc.scalar.dma_start(v_s[a][0:100, :].bitcast(I32), picked_s[24 + 4 * a : 124 + 4 * a, :].bitcast(I32))
+        nc.gpsimd.memset(pages[1][:], 0.0)
+        wgs_sb = kept([P, S], F32, "wgs_sb", after="tab_s")
+        nc.sync.dma_start(wgs_sb[:], wgs)
+
+        w1_w = [kept([P, PACK, P, 2], U8, "w1_w%d" % a) for a in range(PASSES)]
+        for a in range(PASSES):
+            nc.vector.tensor_copy(w1_w[a][:], w1_raw[:, a, :].rearrange("p (q t b) -> p t q b", t=PACK, b=2))
+        w1_s = kept([P, PASSES, PACK, P], U8, "w1_s")
+        nc.vector.tensor_copy(w1_s[:], w1_s_raw[:].rearrange("p a (q t) -> p a t q", t=PACK))
+
+        v_w = [[kept([P, BANK], U32, "v_w%d_%d" % (a, h)) for h in range(HALVES)] for a in range(PASSES)]
+        acc = [[psum.tile([P, BANK], F32, name="acc%d_%d" % (t, h), tag="bank") for h in range(HALVES)] for t in range(PACK)]
+        h_sb = [kept([P, S], F32, "h%d" % t) for t in range(PACK)]
+        cols16 = BANK // 16
+        for a in range(PASSES):
+            for h in range(HALVES):
+                nc.vector.tensor_copy(v_w[a][h][:], tab_w[a][:].bitcast(U32).indirect(idx[:, h * cols16 : (h + 1) * cols16]))
+                for t in range(PACK):
+                    nc.tensor.matmul_mx(
+                        out=acc[t][h][:],
+                        lhsT=w1_w[a][:, t].rearrange("p q b -> p (q b)").bitcast(FP4X4),
+                        lhsT_scale=w1_s[:, a, t, :],
+                        rhs=v_w[a][h][:].bitcast(FP8X4),
+                        rhs_scale=v_s[a][:, h * BANK : (h + 1) * BANK],
+                        start=(a == 0),
+                        stop=(a == PASSES - 1),
+                    )
+                    if a == PASSES - 1:
+                        nc.scalar.activation(h_sb[t][:, h * BANK : (h + 1) * BANK], acc[t][h][:], ACT.Copy, scale=gain_sb[:, t : t + 1])
+
+        wgt_sb = kept([P, M], F32, "wgt_sb", after="w1_raw")
+        nc.sync.dma_start(wgt_sb[:], wgt)
+        flex_all = kept([P, PACK, M], F32, "flex_all", after="tab_w0")
+        nc.sync.dma_start(flex_all[:], flex.rearrange("(p t) m -> p t m", t=PACK))
+        flex_sb = [flex_all[:, 0:2, :], flex_all[:, 2:4, :]]
+        w_both = kept([P, 2, PACK, N], F32, "w_both", after="tab_w1")
+        w_raw = [w_both[:, 0], w_both[:, 1]]
+        for i, w in enumerate((wa, wb)):
+            nc.sync.dma_start(w_raw[i], w.rearrange("(p t) n -> p t n", t=PACK))
+        wc_w = kept([P, N], I32, "wc_w", after="w1_s_raw")
+        nc.sync.dma_start(wc_w[:], wc_words[0].rearrange("p n t -> p (n t)").bitcast(I32))
+        wc_s = kept([P, N], U8, "wc_s", after="picked_s")
+        nc.gpsimd.memset(wc_s[:].bitcast(I32), 0)
+        for q in range(4):
+            nc.sync.dma_start(wc_s[32 * q : 32 * q + 4, :].bitcast(I32), wc_scales[0, 4 * q : 4 * q + 4, :].bitcast(I32))
+
+        w_bf = kept([P, 2, N, PACK], BF16, "w_bf")
+        for i in range(2):
+            nc.scalar.copy(
+                w_bf[:, i].rearrange("p (c i) t -> p c t i", i=4),
+                w_raw[i].rearrange("p t (c i) -> p c t i", i=4),
+            )
+
+        def put(t, lo, hi):
+            nc.vector.tensor_tensor(
+                pages[t % 2][:].indirect(idx2[:, lo // 16 : hi // 16]), h_sb[t][:, lo:hi], wgs_sb[:, lo:hi], ALU.mult
+            )
+
+        def pick(dst, t, lo, hi):
+            nc.vector.tensor_tensor(dst, pages[t % 2][:].indirect(idx3[:, lo // 16 : hi // 16]), wgt_sb[:, lo:hi], ALU.mult)
+
+        starts = [sum(CHUNKS[:c]) for c in range(len(CHUNKS))]
+        pairs = [kept([P, 2, width, 2], BF16, "pairs%d" % c) for c, width in enumerate(CHUNKS)]
+
+        def add_flex(c, u, x):
+            lo, hi = starts[c], starts[c] + CHUNKS[c]
+            nc.vector.tensor_tensor(
+                pairs[c][:, u], x.rearrange("p e m -> p m e"), flex_sb[u][:, :, lo:hi].rearrange("p e m -> p m e"), ALU.add
+            )
+
+        for h in range(HALVES):
+            for t in range(2):
+                put(t, h * BANK, (h + 1) * BANK)
+        x01 = kept([P, 2, M], F32, "x01")
+        for t in range(2):
+            pick(x01[:, t, :], t, 0, M)
+        put(2, 0, S)
+        for c in range(len(CHUNKS)):
+            add_flex(c, 0, x01[:, :, starts[c] : starts[c] + CHUNKS[c]])
+        w_codes = kept([P, 2 * N], U32, "w_codes")
+        w_scale = kept([P, 2 * N], U8, "w_scale")
+        w_flat = w_bf[:].rearrange("p i n t -> p (i n t)")
+        for lo, hi in ((0, 512), (512, 2 * N)):
+            nc.vector.quantize_mx(out=w_codes[:, lo:hi].bitcast(FP8X4), scales=w_scale[:, lo:hi], in_=w_flat[:, PACK * lo : PACK * hi])
+        put(3, 0, S)
+
+        out_rows = out.rearrange("(b p) m -> p b m", p=P)
+        x23 = {}
+        z_bf = {}
+        z_q = {}
+        parts = {}
+
+        def pick_chunk(c):
+            x23[c] = ring.tile([P, 2, CHUNKS[c]], F32, name="x23")
+            for e in range(2):
+                pick(x23[c][:, e, :], 2 + e, starts[c], starts[c] + CHUNKS[c])
+
+        def weave(c):
+            add_flex(c, 1, x23[c][:])
+            z_bf[c] = ring.tile([P, CHUNKS[c], 2], F32, name="z_bf", align_bytes=64)
+            nc.scalar.copy(
+                z_bf[c][:], pairs[c][:].rearrange("p u m e -> p (u m e)").bitcast(F32).rearrange("p (u m) -> p m u", u=2)
+            )
+
+        def quantize(c):
+            codes = ring.tile([P, CHUNKS[c]], U32, name="z_codes", align_bytes=64)
+            scale = ring.tile([P, CHUNKS[c]], U8, name="z_scale", align_bytes=64)
+            nc.vector.quantize_mx(
+                out=codes[:].bitcast(FP8X4), scales=scale[:], in_=z_bf[c][:].rearrange("p m u -> p (m u)").bitcast(BF16)
+            )
+            for lo in range(0, CHUNKS[c], SUB):
+                banks = [psum.tile([P, NB, SUB], F32, name="y%d" % i, tag="bank") for i in range(3)]
+                for i in (0, 2, 1):
+                    for b in range(NB):
+                        if i < 2:
+                            cols = slice(i * N + b * P, i * N + (b + 1) * P)
+                            lhs, lhs_scale = w_codes[:, cols], w_scale[:, cols]
+                        else:
+                            lhs, lhs_scale = wc_w[:, b * P : (b + 1) * P], wc_s[:, b * P : (b + 1) * P]
+                        nc.tensor.matmul_mx(
+                            out=banks[i][:, b, :],
+                            lhsT=lhs.bitcast(FP8X4),
+                            lhsT_scale=lhs_scale,
+                            rhs=codes[:, lo : lo + SUB].bitcast(FP8X4),
+                            rhs_scale=scale[:, lo : lo + SUB],
+                            start=True,
+                            stop=True,
+                        )
+                ya = ring.tile([P, NB, SUB], F32, name="ya", bufs=4)
+                nc.scalar.copy(ya[:], banks[0][:])
+                yc = ring.tile([P, NB, SUB], F32, name="yc", bufs=4)
+                nc.scalar.activation(yc[:], banks[2][:], ACT.Abs)
+                parts[c, lo] = (ya, banks[1], yc)
+
+        best = {}
+
+        def larger(c):
+            for lo in range(0, CHUNKS[c], SUB):
+                ya, yb, yc = parts[c, lo]
+                best[c, lo] = ring.tile([P, NB, SUB], F32, name="best", bufs=4)
+                nc.vector.tensor_tensor(best[c, lo][:], yb[:], ya[:], ALU.max)
+
+        def finish(c):
+            for lo in range(0, CHUNKS[c], SUB):
+                res = ring.tile([P, NB, SUB], F32, name="res", bufs=4)
+                nc.vector.tensor_tensor(res[:], best[c, lo][:], parts[c, lo][2][:], ALU.subtract)
+                nc.sync.dma_start(out_rows[:, :, starts[c] + lo : starts[c] + lo + SUB], res[:])
+
+        last = len(CHUNKS)
+        for step in range(last + 2):
+            if step < last:
+                pick_chunk(step)
+            if 0 <= step - 2:
+                larger(step - 2)
+            if step < last:
+                weave(step)
+            if 0 <= step - 1 < last:
+                quantize(step - 1)
+            if 0 <= step - 2:
+                finish(step - 2)

@@ -1,6 +1,7 @@
 from contextlib import ExitStack
 
 import concourse.mybir as mybir
+from concourse.masks import make_identity
 
 K, H, N, T, S, M, T2 = 1024, 512, 384, 4096, 1024, 1024, 2048
 FLOPS = 2 * K * H * S + 3 * 2 * H * N * M
@@ -70,34 +71,42 @@ def tile_list_brace_pad_scores_kernel(
         gain_sb = kept([P, PACK], F32, "gain_sb")
         nc.gpsimd.dma_start(gain_sb[:], gain.rearrange("(p t) -> p t", t=PACK))
 
-        pages = [kept([P, T2], F32, "page%d" % i) for i in range(2)]
-        nc.gpsimd.memset(pages[0][:], 0.0)
+        ident = kept([P, P], F32, "ident")
+        make_identity(nc, ident[:])
 
         picked_s = kept([P, S], U8, "picked_s")
         nc.vector.tensor_copy(picked_s[:], tab_s[:].bitcast(U8).indirect(idx[:]))
         for a in range(PASSES):
             nc.scalar.dma_start(v_s[a][0:100, :].bitcast(I32), picked_s[24 + 4 * a : 124 + 4 * a, :].bitcast(I32))
-        nc.gpsimd.memset(pages[1][:], 0.0)
         wgs_sb = kept([P, S], F32, "wgs_sb", after="tab_s")
         nc.sync.dma_start(wgs_sb[:], wgs)
 
-        w1_w = [kept([P, PACK, P, 2], U8, "w1_w%d" % a) for a in range(PASSES)]
-        for a in range(PASSES):
-            nc.vector.tensor_copy(w1_w[a][:], w1_raw[:, a, :].rearrange("p (q t b) -> p t q b", t=PACK, b=2))
-        w1_s = kept([P, PASSES, PACK, P], U8, "w1_s")
-        nc.vector.tensor_copy(w1_s[:], w1_s_raw[:].rearrange("p a (q t) -> p a t q", t=PACK))
+        w1_w = kept([P, PASSES, PACK, P], U16, "w1_w")
+        nc.vector.tensor_copy(w1_w[:], w1_raw[:].bitcast(U16).rearrange("p a (q t) -> p a t q", t=PACK))
+        pages = [kept([P, T2], F32, "page0", after="w1_raw")]
+        nc.gpsimd.memset(pages[0][:], 0.0)
 
         v_w = [[kept([P, BANK], U32, "v_w%d_%d" % (a, h)) for h in range(HALVES)] for a in range(PASSES)]
         acc = [[psum.tile([P, BANK], F32, name="acc%d_%d" % (t, h), tag="bank") for h in range(HALVES)] for t in range(PACK)]
         h_sb = [kept([P, S], F32, "h%d" % t) for t in range(PACK)]
         cols16 = BANK // 16
-        for a in range(PASSES):
-            for h in range(HALVES):
-                nc.vector.tensor_copy(v_w[a][h][:], tab_w[a][:].bitcast(U32).indirect(idx[:, h * cols16 : (h + 1) * cols16]))
-                for t in range(PACK):
+
+        def pick_words(a, h):
+            nc.vector.tensor_copy(v_w[a][h][:], tab_w[a][:].bitcast(U32).indirect(idx[:, h * cols16 : (h + 1) * cols16]))
+
+        for h in range(HALVES):
+            pick_words(0, h)
+        w1_s = kept([P, PASSES, PACK, P], U8, "w1_s", after="tab_w0")
+        nc.vector.tensor_copy(w1_s[:], w1_s_raw[:].rearrange("p a (q t) -> p a t q", t=PACK))
+        pages.append(kept([P, T2], F32, "page1", after="w1_s_raw"))
+        nc.gpsimd.memset(pages[1][:], 0.0)
+        for h in range(HALVES):
+            pick_words(1, h)
+            for t in range(PACK):
+                for a in range(PASSES):
                     nc.tensor.matmul_mx(
                         out=acc[t][h][:],
-                        lhsT=w1_w[a][:, t].rearrange("p q b -> p (q b)").bitcast(FP4X4),
+                        lhsT=w1_w[:, a, t, :].bitcast(FP4X4),
                         lhsT_scale=w1_s[:, a, t, :],
                         rhs=v_w[a][h][:].bitcast(FP8X4),
                         rhs_scale=v_s[a][:, h * BANK : (h + 1) * BANK],
@@ -107,7 +116,7 @@ def tile_list_brace_pad_scores_kernel(
                     if a == PASSES - 1:
                         nc.scalar.activation(h_sb[t][:, h * BANK : (h + 1) * BANK], acc[t][h][:], ACT.Copy, scale=gain_sb[:, t : t + 1])
 
-        wgt_sb = kept([P, M], F32, "wgt_sb", after="w1_raw")
+        wgt_sb = kept([P, M], F32, "wgt_sb", after="v_w0_0")
         nc.sync.dma_start(wgt_sb[:], wgt)
         flex_all = kept([P, PACK, M], F32, "flex_all", after="tab_w0")
         nc.sync.dma_start(flex_all[:], flex.rearrange("(p t) m -> p t m", t=PACK))
@@ -116,7 +125,7 @@ def tile_list_brace_pad_scores_kernel(
         w_raw = [w_both[:, 0], w_both[:, 1]]
         for i, w in enumerate((wa, wb)):
             nc.sync.dma_start(w_raw[i], w.rearrange("(p t) n -> p t n", t=PACK))
-        wc_w = kept([P, N], I32, "wc_w", after="w1_s_raw")
+        wc_w = kept([P, N], I32, "wc_w", after="v_w0_1")
         nc.sync.dma_start(wc_w[:], wc_words[0].rearrange("p n t -> p (n t)").bitcast(I32))
         wc_s = kept([P, N], U8, "wc_s", after="picked_s")
         nc.gpsimd.memset(wc_s[:].bitcast(I32), 0)
@@ -141,11 +150,12 @@ def tile_list_brace_pad_scores_kernel(
         starts = [sum(CHUNKS[:c]) for c in range(len(CHUNKS))]
         pairs = [kept([P, 2, width, 2], BF16, "pairs%d" % c) for c, width in enumerate(CHUNKS)]
 
+        flex23 = kept([P, M, 2], F32, "flex23")
+        nc.scalar.copy(flex23[:], flex_sb[1].rearrange("p e m -> p m e"))
+
         def add_flex(c, u, x):
             lo, hi = starts[c], starts[c] + CHUNKS[c]
-            nc.vector.tensor_tensor(
-                pairs[c][:, u], x.rearrange("p e m -> p m e"), flex_sb[u][:, :, lo:hi].rearrange("p e m -> p m e"), ALU.add
-            )
+            nc.vector.tensor_tensor(pairs[c][:, u], x.rearrange("p e m -> p m e"), flex23[:, lo:hi, :], ALU.add)
 
         for h in range(HALVES):
             for t in range(2):
@@ -154,8 +164,21 @@ def tile_list_brace_pad_scores_kernel(
         for t in range(2):
             pick(x01[:, t, :], t, 0, M)
         put(2, 0, S)
-        for c in range(len(CHUNKS)):
-            add_flex(c, 0, x01[:, :, starts[c] : starts[c] + CHUNKS[c]])
+        turned = kept([P, M // P, P, 2], BF16, "turned")
+        for j0 in range(0, M // P, 2):
+            bank = psum.tile([P, 2, 2, P], F32, name="sum_t", tag="bank")
+            for j in range(2):
+                cols = slice((j0 + j) * P, (j0 + j + 1) * P)
+                for e in range(2):
+                    nc.tensor.matmul(bank[:, j, e, :], x01[:, e, cols], ident[:], is_transpose=True, start=True, stop=False)
+                    nc.tensor.matmul(bank[:, j, e, :], flex_sb[0][:, e, cols], ident[:], is_transpose=True, start=False, stop=True)
+            nc.scalar.copy(turned[:, j0 : j0 + 2], bank[:].rearrange("m j e p -> m j p e"))
+        for c, width in enumerate(CHUNKS):
+            bank = psum.tile([P, width], F32, name="back", tag="bank")
+            for lo in range(0, width, P):
+                words = turned[:, (starts[c] + lo) // P].rearrange("m p e -> m (p e)").bitcast(F32)
+                nc.tensor.transpose(bank[:, lo : lo + P], words, ident[:])
+            nc.scalar.copy(pairs[c][:, 0].rearrange("p m e -> p (m e)").bitcast(F32), bank[:])
         w_codes = kept([P, 2 * N], U32, "w_codes")
         w_scale = kept([P, 2 * N], U8, "w_scale")
         w_flat = w_bf[:].rearrange("p i n t -> p (i n t)")

@@ -24,7 +24,7 @@ BANK = 512
 HALVES = S // BANK
 NB = N // P
 SUB = 128
-CHUNKS = (256, 256, 256, 128, 128)
+CHUNKS = (256, 256, 256, 256)
 
 
 def tile_list_brace_pad_scores_kernel(
@@ -36,28 +36,30 @@ def tile_list_brace_pad_scores_kernel(
         lists = ctx.enter_context(tc.tile_pool(name="lists", bufs=1))
         keep = ctx.enter_context(tc.tile_pool(name="keep", bufs=1))
         ring = ctx.enter_context(tc.tile_pool(name="ring", bufs=2))
-        psum = ctx.enter_context(tc.psum_pool(name="psum", bufs=8))
+        psum = ctx.enter_context(tc.psum_pool(name="psum", bufs=6))
 
         def kept(shape, dtype, name, after=None):
             return keep.tile(shape, dtype, name=name, tag=after or name, align_bytes=64)
 
         tab_s = kept([P, T // 4], I32, "tab_s")
-        for q in range(4):
-            nc.vector.memset(tab_s[32 * q : 32 * q + 24, :], 0)
+        nc.vector.memset(tab_s[0:96, :], 0)
         w1_s_raw = kept([P, PASSES, H], U8, "w1_s_raw")
         nc.gpsimd.memset(w1_s_raw[:].rearrange("p a c -> p (a c)").bitcast(I32), 0)
         v_s = [kept([P, S], U8, "v_s%d" % a) for a in range(PASSES)]
         for a in range(PASSES):
             nc.vector.memset(v_s[a][:].bitcast(I32), 0)
+        page1 = kept([P, T2], F32, "page1")
+        nc.vector.memset(page1[:], 0.0)
 
         idx = lists.tile([P, S // 16], U16, name="idx")
         idx2 = lists.tile([P, S // 16], U16, name="idx2")
         idx3 = lists.tile([P, M // 16], U16, name="idx3")
         nc.sync.dma_start(idx[:], offs)
-        for q in range(4):
-            nc.sync.dma_start(tab_s[32 * q + 24 : 32 * q + 32, :], tab_scales[:, 4 * q : 4 * q + 4, :].bitcast(I32))
+        nc.sync.dma_start(tab_s[96:128, :], tab_scales.rearrange("a q t -> (a q) t").bitcast(I32))
         w1_raw = kept([P, PASSES, 2 * H], U8, "w1_raw")
         nc.sync.dma_start(w1_raw[:].bitcast(I32), w1_words.rearrange("a p c -> p a c").bitcast(I32))
+        nc.sync.dma_start(idx2[:], offs2)
+        nc.sync.dma_start(idx3[:], offs3)
         tab_w = [kept([P, T], I32, "tab_w%d" % a) for a in range(PASSES)]
         for a in range(PASSES):
             nc.sync.dma_start(tab_w[a][:], tab_words[a].rearrange("p n t -> p (n t)").bitcast(I32))
@@ -66,8 +68,8 @@ def tile_list_brace_pad_scores_kernel(
                 w1_s_raw[32 * q : 32 * q + 4, :, :].bitcast(I32),
                 w1_scales[:, 4 * q : 4 * q + 4, :].rearrange("a r c -> r a c").bitcast(I32),
             )
-        nc.sync.dma_start(idx2[:], offs2)
-        nc.sync.dma_start(idx3[:], offs3)
+        wgs_sb = kept([P, S], F32, "wgs_sb")
+        nc.sync.dma_start(wgs_sb[:], wgs)
         gain_sb = kept([P, PACK], F32, "gain_sb")
         nc.gpsimd.dma_start(gain_sb[:], gain.rearrange("(p t) -> p t", t=PACK))
 
@@ -77,17 +79,17 @@ def tile_list_brace_pad_scores_kernel(
         picked_s = kept([P, S], U8, "picked_s")
         nc.vector.tensor_copy(picked_s[:], tab_s[:].bitcast(U8).indirect(idx[:]))
         for a in range(PASSES):
-            nc.scalar.dma_start(v_s[a][0:100, :].bitcast(I32), picked_s[24 + 4 * a : 124 + 4 * a, :].bitcast(I32))
-        wgs_sb = kept([P, S], F32, "wgs_sb", after="tab_s")
-        nc.sync.dma_start(wgs_sb[:], wgs)
+            for q in range(4):
+                queue = nc.scalar if q < 3 else nc.gpsimd
+                row = 96 + 16 * a + 4 * q
+                queue.dma_start(v_s[a][32 * q : 32 * q + 4, :].bitcast(I32), picked_s[row : row + 4, :].bitcast(I32))
 
         w1_w = kept([P, PASSES, PACK, P], U16, "w1_w")
         nc.vector.tensor_copy(w1_w[:], w1_raw[:].bitcast(U16).rearrange("p a (q t) -> p a t q", t=PACK))
-        pages = [kept([P, T2], F32, "page0", after="w1_raw")]
-        nc.gpsimd.memset(pages[0][:], 0.0)
+        pages = [kept([P, T2], F32, "page0", after="w1_raw"), page1]
+        nc.vector.memset(pages[0][:], 0.0)
 
         v_w = [[kept([P, BANK], U32, "v_w%d_%d" % (a, h)) for h in range(HALVES)] for a in range(PASSES)]
-        acc = [[psum.tile([P, BANK], F32, name="acc%d_%d" % (t, h), tag="bank") for h in range(HALVES)] for t in range(PACK)]
         h_sb = [kept([P, S], F32, "h%d" % t) for t in range(PACK)]
         cols16 = BANK // 16
 
@@ -98,23 +100,23 @@ def tile_list_brace_pad_scores_kernel(
             pick_words(0, h)
         w1_s = kept([P, PASSES, PACK, P], U8, "w1_s", after="tab_w0")
         nc.vector.tensor_copy(w1_s[:], w1_s_raw[:].rearrange("p a (q t) -> p a t q", t=PACK))
-        pages.append(kept([P, T2], F32, "page1", after="w1_s_raw"))
-        nc.gpsimd.memset(pages[1][:], 0.0)
         for h in range(HALVES):
             pick_words(1, h)
-            for t in range(PACK):
-                for a in range(PASSES):
-                    nc.tensor.matmul_mx(
-                        out=acc[t][h][:],
-                        lhsT=w1_w[:, a, t, :].bitcast(FP4X4),
-                        lhsT_scale=w1_s[:, a, t, :],
-                        rhs=v_w[a][h][:].bitcast(FP8X4),
-                        rhs_scale=v_s[a][:, h * BANK : (h + 1) * BANK],
-                        start=(a == 0),
-                        stop=(a == PASSES - 1),
-                    )
-                    if a == PASSES - 1:
-                        nc.scalar.activation(h_sb[t][:, h * BANK : (h + 1) * BANK], acc[t][h][:], ACT.Copy, scale=gain_sb[:, t : t + 1])
+        for u in range(2):
+            for h in range(HALVES):
+                for t in (2 * u, 2 * u + 1):
+                    acc = psum.tile([P, BANK], F32, name="acc", tag="quick", bufs=2)
+                    for a in range(PASSES):
+                        nc.tensor.matmul_mx(
+                            out=acc[:],
+                            lhsT=w1_w[:, a, t, :].bitcast(FP4X4),
+                            lhsT_scale=w1_s[:, a, t, :],
+                            rhs=v_w[a][h][:].bitcast(FP8X4),
+                            rhs_scale=v_s[a][:, h * BANK : (h + 1) * BANK],
+                            start=(a == 0),
+                            stop=(a == PASSES - 1),
+                        )
+                    nc.scalar.activation(h_sb[t][:, h * BANK : (h + 1) * BANK], acc[:], ACT.Copy, scale=gain_sb[:, t : t + 1])
 
         wgt_sb = kept([P, M], F32, "wgt_sb", after="v_w0_0")
         nc.sync.dma_start(wgt_sb[:], wgt)
@@ -127,7 +129,7 @@ def tile_list_brace_pad_scores_kernel(
             nc.sync.dma_start(w_raw[i], w.rearrange("(p t) n -> p t n", t=PACK))
         wc_w = kept([P, N], I32, "wc_w", after="v_w0_1")
         nc.sync.dma_start(wc_w[:], wc_words[0].rearrange("p n t -> p (n t)").bitcast(I32))
-        wc_s = kept([P, N], U8, "wc_s", after="picked_s")
+        wc_s = kept([P, N], U8, "wc_s", after="v_w1_0")
         nc.gpsimd.memset(wc_s[:].bitcast(I32), 0)
         for q in range(4):
             nc.sync.dma_start(wc_s[32 * q : 32 * q + 4, :].bitcast(I32), wc_scales[0, 4 * q : 4 * q + 4, :].bitcast(I32))
@@ -193,13 +195,13 @@ def tile_list_brace_pad_scores_kernel(
         parts = {}
 
         def pick_chunk(c):
-            x23[c] = ring.tile([P, 2, CHUNKS[c]], F32, name="x23")
+            x23[c] = kept([P, 2, CHUNKS[c]], F32, "x23_%d" % c, after="z_bf%d" % (c - 2) if c >= 2 else None)
             for e in range(2):
                 pick(x23[c][:, e, :], 2 + e, starts[c], starts[c] + CHUNKS[c])
 
         def weave(c):
             add_flex(c, 1, x23[c][:])
-            z_bf[c] = ring.tile([P, CHUNKS[c], 2], F32, name="z_bf", align_bytes=64)
+            z_bf[c] = kept([P, CHUNKS[c], 2], F32, "z_bf%d" % c)
             nc.scalar.copy(
                 z_bf[c][:], pairs[c][:].rearrange("p u m e -> p (u m e)").bitcast(F32).rearrange("p (u m) -> p m u", u=2)
             )
@@ -210,8 +212,15 @@ def tile_list_brace_pad_scores_kernel(
             nc.vector.quantize_mx(
                 out=codes[:].bitcast(FP8X4), scales=scale[:], in_=z_bf[c][:].rearrange("p m u -> p (m u)").bitcast(BF16)
             )
+            ya = ring.tile([P, NB, CHUNKS[c]], F32, name="ya", bufs=3)
+            yc = ring.tile([P, NB, CHUNKS[c]], F32, name="yc", bufs=3)
+            yb = []
             for lo in range(0, CHUNKS[c], SUB):
-                banks = [psum.tile([P, NB, SUB], F32, name="y%d" % i, tag="bank") for i in range(3)]
+                banks = [
+                    psum.tile([P, NB, SUB], F32, name="y_a", tag="quick", bufs=2),
+                    psum.tile([P, NB, SUB], F32, name="y_b", tag="bank"),
+                    psum.tile([P, NB, SUB], F32, name="y_c", tag="quick", bufs=2),
+                ]
                 for i in (0, 2, 1):
                     for b in range(NB):
                         if i < 2:
@@ -228,35 +237,38 @@ def tile_list_brace_pad_scores_kernel(
                             start=True,
                             stop=True,
                         )
-                ya = ring.tile([P, NB, SUB], F32, name="ya", bufs=4)
-                nc.scalar.copy(ya[:], banks[0][:])
-                yc = ring.tile([P, NB, SUB], F32, name="yc", bufs=4)
-                nc.scalar.activation(yc[:], banks[2][:], ACT.Abs)
-                parts[c, lo] = (ya, banks[1], yc)
+                nc.scalar.copy(ya[:, :, lo : lo + SUB], banks[0][:])
+                nc.scalar.activation(yc[:, :, lo : lo + SUB], banks[2][:], ACT.Abs)
+                yb.append(banks[1])
+            parts[c] = (ya, yb, yc)
 
         best = {}
 
         def larger(c):
-            for lo in range(0, CHUNKS[c], SUB):
-                ya, yb, yc = parts[c, lo]
-                best[c, lo] = ring.tile([P, NB, SUB], F32, name="best", bufs=4)
-                nc.vector.tensor_tensor(best[c, lo][:], yb[:], ya[:], ALU.max)
+            ya, yb, yc = parts[c]
+            best[c] = ring.tile([P, NB, CHUNKS[c]], F32, name="best")
+            for i, lo in enumerate(range(0, CHUNKS[c], SUB)):
+                nc.vector.tensor_tensor(best[c][:, :, lo : lo + SUB], yb[i][:], ya[:, :, lo : lo + SUB], ALU.max)
 
         def finish(c):
-            for lo in range(0, CHUNKS[c], SUB):
-                res = ring.tile([P, NB, SUB], F32, name="res", bufs=4)
-                nc.vector.tensor_tensor(res[:], best[c, lo][:], parts[c, lo][2][:], ALU.subtract)
-                nc.sync.dma_start(out_rows[:, :, starts[c] + lo : starts[c] + lo + SUB], res[:])
+            width = SUB if c == len(CHUNKS) - 1 else CHUNKS[c]
+            for lo in range(0, CHUNKS[c], width):
+                res = ring.tile([P, NB, width], F32, name="res", bufs=3)
+                nc.vector.tensor_tensor(res[:], best[c][:, :, lo : lo + width], parts[c][2][:, :, lo : lo + width], ALU.subtract)
+                nc.sync.dma_start(out_rows[:, :, starts[c] + lo : starts[c] + lo + width], res[:])
 
         last = len(CHUNKS)
-        for step in range(last + 2):
-            if step < last:
-                pick_chunk(step)
-            if 0 <= step - 2:
-                larger(step - 2)
+        pick_chunk(0)
+        for step in range(last + 1):
             if step < last:
                 weave(step)
-            if 0 <= step - 1 < last:
-                quantize(step - 1)
-            if 0 <= step - 2:
-                finish(step - 2)
+            if step == 0:
+                pick_chunk(1)
+            if step >= 1:
+                larger(step - 1)
+            if step < last:
+                quantize(step)
+            if step >= 1:
+                finish(step - 1)
+            if step + 2 < last:
+                pick_chunk(step + 2)

@@ -43,11 +43,11 @@ def tile_list_brace_pad_scores_kernel(
 
         tab_s = kept([P, T // 4], I32, "tab_s")
         nc.vector.memset(tab_s[0:96, :], 0)
-        w1_s_raw = kept([P, PASSES, H], U8, "w1_s_raw")
-        nc.gpsimd.memset(w1_s_raw[:].rearrange("p a c -> p (a c)").bitcast(I32), 0)
-        v_s = [kept([P, S], U8, "v_s%d" % a) for a in range(PASSES)]
+        w1_s_raw = kept([P, H // 4], I32, "w1_s_raw")
+        nc.vector.memset(w1_s_raw[0:96, :], 0)
+        planes = [kept([P, S + H], U8, "plane%d" % a) for a in range(PASSES)]
         for a in range(PASSES):
-            nc.vector.memset(v_s[a][:].bitcast(I32), 0)
+            nc.vector.memset(planes[a][:].bitcast(I32), 0)
         page1 = kept([P, T2], F32, "page1")
         nc.vector.memset(page1[:], 0.0)
 
@@ -56,6 +56,7 @@ def tile_list_brace_pad_scores_kernel(
         idx3 = lists.tile([P, M // 16], U16, name="idx3")
         nc.sync.dma_start(idx[:], offs)
         nc.sync.dma_start(tab_s[96:128, :], tab_scales.rearrange("a q t -> (a q) t").bitcast(I32))
+        nc.sync.dma_start(w1_s_raw[96:128, :], w1_scales.rearrange("a q c -> (a q) c").bitcast(I32))
         w1_raw = kept([P, PASSES, 2 * H], U8, "w1_raw")
         nc.sync.dma_start(w1_raw[:].bitcast(I32), w1_words.rearrange("a p c -> p a c").bitcast(I32))
         nc.sync.dma_start(idx2[:], offs2)
@@ -63,11 +64,6 @@ def tile_list_brace_pad_scores_kernel(
         tab_w = [kept([P, T], I32, "tab_w%d" % a) for a in range(PASSES)]
         for a in range(PASSES):
             nc.sync.dma_start(tab_w[a][:], tab_words[a].rearrange("p n t -> p (n t)").bitcast(I32))
-        for q in range(4):
-            nc.gpsimd.dma_start(
-                w1_s_raw[32 * q : 32 * q + 4, :, :].bitcast(I32),
-                w1_scales[:, 4 * q : 4 * q + 4, :].rearrange("a r c -> r a c").bitcast(I32),
-            )
         wgs_sb = kept([P, S], F32, "wgs_sb")
         nc.sync.dma_start(wgs_sb[:], wgs)
         gain_sb = kept([P, PACK], F32, "gain_sb")
@@ -78,16 +74,19 @@ def tile_list_brace_pad_scores_kernel(
 
         picked_s = kept([P, S], U8, "picked_s")
         nc.vector.tensor_copy(picked_s[:], tab_s[:].bitcast(U8).indirect(idx[:]))
+        rows = kept([P, S + H], U8, "rows")
+        nc.vector.tensor_copy(rows[:, S:].rearrange("p (t q) -> p t q", t=PACK), w1_s_raw[:].bitcast(U8).rearrange("p (q t) -> p t q", t=PACK))
+        nc.vector.tensor_copy(rows[:, :S].bitcast(I32), picked_s[:].bitcast(I32))
         for a in range(PASSES):
             for q in range(4):
                 queue = nc.scalar if q < 3 else nc.gpsimd
                 row = 96 + 16 * a + 4 * q
-                queue.dma_start(v_s[a][32 * q : 32 * q + 4, :].bitcast(I32), picked_s[row : row + 4, :].bitcast(I32))
+                queue.dma_start(planes[a][32 * q : 32 * q + 4, :].bitcast(I32), rows[row : row + 4, :].bitcast(I32))
 
         w1_w = kept([P, PASSES, PACK, P], U16, "w1_w")
         nc.vector.tensor_copy(w1_w[:], w1_raw[:].bitcast(U16).rearrange("p a (q t) -> p a t q", t=PACK))
         pages = [kept([P, T2], F32, "page0", after="w1_raw"), page1]
-        nc.vector.memset(pages[0][:], 0.0)
+        nc.gpsimd.memset(pages[0][:], 0.0)
 
         v_w = [[kept([P, BANK], U32, "v_w%d_%d" % (a, h)) for h in range(HALVES)] for a in range(PASSES)]
         h_sb = [kept([P, S], F32, "h%d" % t) for t in range(PACK)]
@@ -98,25 +97,32 @@ def tile_list_brace_pad_scores_kernel(
 
         for h in range(HALVES):
             pick_words(0, h)
-        w1_s = kept([P, PASSES, PACK, P], U8, "w1_s", after="tab_w0")
-        nc.vector.tensor_copy(w1_s[:], w1_s_raw[:].rearrange("p a (q t) -> p a t q", t=PACK))
         for h in range(HALVES):
             pick_words(1, h)
-        for u in range(2):
-            for h in range(HALVES):
-                for t in (2 * u, 2 * u + 1):
-                    acc = psum.tile([P, BANK], F32, name="acc", tag="quick", bufs=2)
-                    for a in range(PASSES):
-                        nc.tensor.matmul_mx(
-                            out=acc[:],
-                            lhsT=w1_w[:, a, t, :].bitcast(FP4X4),
-                            lhsT_scale=w1_s[:, a, t, :],
-                            rhs=v_w[a][h][:].bitcast(FP8X4),
-                            rhs_scale=v_s[a][:, h * BANK : (h + 1) * BANK],
-                            start=(a == 0),
-                            stop=(a == PASSES - 1),
-                        )
-                    nc.scalar.activation(h_sb[t][:, h * BANK : (h + 1) * BANK], acc[:], ACT.Copy, scale=gain_sb[:, t : t + 1])
+
+        def features(t, lo, hi, step):
+            acc = psum.tile([P, hi - lo], F32, name="acc", tag="quick", bufs=2)
+            h = lo // BANK
+            for c in range(lo, hi, step):
+                for a in range(PASSES):
+                    nc.tensor.matmul_mx(
+                        out=acc[:, c - lo : c - lo + step],
+                        lhsT=w1_w[:, a, t, :].bitcast(FP4X4),
+                        lhsT_scale=planes[a][:, S + t * P : S + (t + 1) * P],
+                        rhs=v_w[a][h][:, c - h * BANK : c - h * BANK + step].bitcast(FP8X4),
+                        rhs_scale=planes[a][:, c : c + step],
+                        start=(a == 0),
+                        stop=(a == PASSES - 1),
+                    )
+            nc.scalar.activation(h_sb[t][:, lo:hi], acc[:], ACT.Copy, scale=gain_sb[:, t : t + 1])
+
+        first_runs = ((0, P, P), (P, BANK, P), (BANK, S, BANK))
+        for lo, hi, step in first_runs:
+            for t in range(2):
+                features(t, lo, hi, step)
+        for h in range(HALVES):
+            for t in range(2, PACK):
+                features(t, h * BANK, (h + 1) * BANK, BANK)
 
         wgt_sb = kept([P, M], F32, "wgt_sb", after="v_w0_0")
         nc.sync.dma_start(wgt_sb[:], wgt)
@@ -159,9 +165,9 @@ def tile_list_brace_pad_scores_kernel(
             lo, hi = starts[c], starts[c] + CHUNKS[c]
             nc.vector.tensor_tensor(pairs[c][:, u], x.rearrange("p e m -> p m e"), flex23[:, lo:hi, :], ALU.add)
 
-        for h in range(HALVES):
+        for lo, hi, step in first_runs:
             for t in range(2):
-                put(t, h * BANK, (h + 1) * BANK)
+                put(t, lo, hi)
         x01 = kept([P, 2, M], F32, "x01")
         for t in range(2):
             pick(x01[:, t, :], t, 0, M)

from contextlib import ExitStack

import concourse.mybir as mybir
from concourse.masks import make_identity

K, H, N, T, S, M, T2 = 1024, 512, 384, 4096, 1024, 1024, 2048
FLOPS = 2 * K * H * S + 3 * 2 * H * N * M

F32 = mybir.dt.float32
BF16 = mybir.dt.bfloat16
I32 = mybir.dt.int32
U32 = mybir.dt.uint32
U16 = mybir.dt.uint16
U8 = mybir.dt.uint8
FP8X4 = mybir.dt.float8_e4m3fn_x4
FP4X4 = mybir.dt.float4_e2m1fn_x4
ALU = mybir.AluOpType
ACT = mybir.ActivationFunctionType

P = 128
PACK = 4
PASSES = K // (P * PACK)
BANK = 512
HALVES = S // BANK
NB = N // P
SUB = 128
CHUNKS = (256, 256, 256, 256)


def tile_list_brace_pad_scores_kernel(
    tc, tab_words, tab_scales, offs, offs2, offs3, w1_words, w1_scales, gain, wgs, wgt, flex, wa, wb,
    wc_words, wc_scales, out,
):
    nc = tc.nc
    with ExitStack() as ctx:
        lists = ctx.enter_context(tc.tile_pool(name="lists", bufs=1))
        keep = ctx.enter_context(tc.tile_pool(name="keep", bufs=1))
        ring = ctx.enter_context(tc.tile_pool(name="ring", bufs=2))
        psum = ctx.enter_context(tc.psum_pool(name="psum", bufs=6))

        def kept(shape, dtype, name, after=None):
            return keep.tile(shape, dtype, name=name, tag=after or name, align_bytes=64)

        tab_s = kept([P, T // 4], I32, "tab_s")
        nc.vector.memset(tab_s[0:96, :], 0)
        w1_s_raw = kept([P, H // 4], I32, "w1_s_raw")
        nc.vector.memset(w1_s_raw[0:96, :], 0)
        planes = [kept([P, S + H], U8, "plane%d" % a) for a in range(PASSES)]
        for a in range(PASSES):
            nc.vector.memset(planes[a][:].bitcast(I32), 0)
        page1 = kept([P, T2], F32, "page1")
        nc.vector.memset(page1[:], 0.0)

        idx = lists.tile([P, S // 16], U16, name="idx")
        idx2 = lists.tile([P, S // 16], U16, name="idx2")
        idx3 = lists.tile([P, M // 16], U16, name="idx3")
        nc.sync.dma_start(idx[:], offs)
        nc.sync.dma_start(tab_s[96:128, :], tab_scales.rearrange("a q t -> (a q) t").bitcast(I32))
        nc.sync.dma_start(w1_s_raw[96:128, :], w1_scales.rearrange("a q c -> (a q) c").bitcast(I32))
        w1_raw = kept([P, PASSES, 2 * H], U8, "w1_raw")
        nc.sync.dma_start(w1_raw[:].bitcast(I32), w1_words.rearrange("a p c -> p a c").bitcast(I32))
        nc.sync.dma_start(idx2[:], offs2)
        nc.sync.dma_start(idx3[:], offs3)
        tab_w = [kept([P, T], I32, "tab_w%d" % a) for a in range(PASSES)]
        for a in range(PASSES):
            nc.sync.dma_start(tab_w[a][:], tab_words[a].rearrange("p n t -> p (n t)").bitcast(I32))
        wgs_sb = kept([P, S], F32, "wgs_sb")
        nc.sync.dma_start(wgs_sb[:], wgs)
        gain_sb = kept([P, PACK], F32, "gain_sb")
        nc.gpsimd.dma_start(gain_sb[:], gain.rearrange("(p t) -> p t", t=PACK))

        ident = kept([P, P], F32, "ident")
        make_identity(nc, ident[:])

        picked_s = kept([P, S], U8, "picked_s")
        nc.vector.tensor_copy(picked_s[:], tab_s[:].bitcast(U8).indirect(idx[:]))
        rows = kept([P, S + H], U8, "rows")
        nc.vector.tensor_copy(rows[:, S:].rearrange("p (t q) -> p t q", t=PACK), w1_s_raw[:].bitcast(U8).rearrange("p (q t) -> p t q", t=PACK))
        nc.vector.tensor_copy(rows[:, :S].bitcast(I32), picked_s[:].bitcast(I32))
        for a in range(PASSES):
            for q in range(4):
                queue = nc.scalar if q < 3 else nc.gpsimd
                row = 96 + 16 * a + 4 * q
                queue.dma_start(planes[a][32 * q : 32 * q + 4, :].bitcast(I32), rows[row : row + 4, :].bitcast(I32))

        w1_w = kept([P, PASSES, PACK, P], U16, "w1_w")
        nc.vector.tensor_copy(w1_w[:], w1_raw[:].bitcast(U16).rearrange("p a (q t) -> p a t q", t=PACK))
        pages = [kept([P, T2], F32, "page0", after="w1_raw"), page1]
        nc.gpsimd.memset(pages[0][:], 0.0)

        v_w = [[kept([P, BANK], U32, "v_w%d_%d" % (a, h)) for h in range(HALVES)] for a in range(PASSES)]
        h_sb = [kept([P, S], F32, "h%d" % t) for t in range(PACK)]
        cols16 = BANK // 16

        def pick_words(a, h):
            nc.vector.tensor_copy(v_w[a][h][:], tab_w[a][:].bitcast(U32).indirect(idx[:, h * cols16 : (h + 1) * cols16]))

        for h in range(HALVES):
            pick_words(0, h)
        for h in range(HALVES):
            pick_words(1, h)

        def features(t, lo, hi, step):
            acc = psum.tile([P, hi - lo], F32, name="acc", tag="quick", bufs=2)
            h = lo // BANK
            for c in range(lo, hi, step):
                for a in range(PASSES):
                    nc.tensor.matmul_mx(
                        out=acc[:, c - lo : c - lo + step],
                        lhsT=w1_w[:, a, t, :].bitcast(FP4X4),
                        lhsT_scale=planes[a][:, S + t * P : S + (t + 1) * P],
                        rhs=v_w[a][h][:, c - h * BANK : c - h * BANK + step].bitcast(FP8X4),
                        rhs_scale=planes[a][:, c : c + step],
                        start=(a == 0),
                        stop=(a == PASSES - 1),
                    )
            nc.scalar.activation(h_sb[t][:, lo:hi], acc[:], ACT.Copy, scale=gain_sb[:, t : t + 1])

        first_runs = ((0, P, P), (P, BANK, P), (BANK, S, BANK))
        for lo, hi, step in first_runs:
            for t in range(2):
                features(t, lo, hi, step)
        for h in range(HALVES):
            for t in range(2, PACK):
                features(t, h * BANK, (h + 1) * BANK, BANK)

        wgt_sb = kept([P, M], F32, "wgt_sb", after="v_w0_0")
        nc.sync.dma_start(wgt_sb[:], wgt)
        flex_all = kept([P, PACK, M], F32, "flex_all", after="tab_w0")
        nc.sync.dma_start(flex_all[:], flex.rearrange("(p t) m -> p t m", t=PACK))
        flex_sb = [flex_all[:, 0:2, :], flex_all[:, 2:4, :]]
        w_both = kept([P, 2, PACK, N], F32, "w_both", after="tab_w1")
        w_raw = [w_both[:, 0], w_both[:, 1]]
        for i, w in enumerate((wa, wb)):
            nc.sync.dma_start(w_raw[i], w.rearrange("(p t) n -> p t n", t=PACK))
        wc_w = kept([P, N], I32, "wc_w", after="v_w0_1")
        nc.sync.dma_start(wc_w[:], wc_words[0].rearrange("p n t -> p (n t)").bitcast(I32))
        wc_s = kept([P, N], U8, "wc_s", after="v_w1_0")
        nc.gpsimd.memset(wc_s[:].bitcast(I32), 0)
        for q in range(4):
            nc.sync.dma_start(wc_s[32 * q : 32 * q + 4, :].bitcast(I32), wc_scales[0, 4 * q : 4 * q + 4, :].bitcast(I32))

        w_bf = kept([P, 2, N, PACK], BF16, "w_bf")
        for i in range(2):
            nc.scalar.copy(
                w_bf[:, i].rearrange("p (c i) t -> p c t i", i=4),
                w_raw[i].rearrange("p t (c i) -> p c t i", i=4),
            )

        def put(t, lo, hi):
            nc.vector.tensor_tensor(
                pages[t % 2][:].indirect(idx2[:, lo // 16 : hi // 16]), h_sb[t][:, lo:hi], wgs_sb[:, lo:hi], ALU.mult
            )

        def pick(dst, t, lo, hi):
            nc.vector.tensor_tensor(dst, pages[t % 2][:].indirect(idx3[:, lo // 16 : hi // 16]), wgt_sb[:, lo:hi], ALU.mult)

        starts = [sum(CHUNKS[:c]) for c in range(len(CHUNKS))]
        pairs = [kept([P, 2, width, 2], BF16, "pairs%d" % c) for c, width in enumerate(CHUNKS)]

        flex23 = kept([P, M, 2], F32, "flex23")
        nc.scalar.copy(flex23[:], flex_sb[1].rearrange("p e m -> p m e"))

        def add_flex(c, u, x):
            lo, hi = starts[c], starts[c] + CHUNKS[c]
            nc.vector.tensor_tensor(pairs[c][:, u], x.rearrange("p e m -> p m e"), flex23[:, lo:hi, :], ALU.add)

        for lo, hi, step in first_runs:
            for t in range(2):
                put(t, lo, hi)
        x01 = kept([P, 2, M], F32, "x01")
        for t in range(2):
            pick(x01[:, t, :], t, 0, M)
        put(2, 0, S)
        turned = kept([P, M // P, P, 2], BF16, "turned")
        for j0 in range(0, M // P, 2):
            bank = psum.tile([P, 2, 2, P], F32, name="sum_t", tag="bank")
            for j in range(2):
                cols = slice((j0 + j) * P, (j0 + j + 1) * P)
                for e in range(2):
                    nc.tensor.matmul(bank[:, j, e, :], x01[:, e, cols], ident[:], is_transpose=True, start=True, stop=False)
                    nc.tensor.matmul(bank[:, j, e, :], flex_sb[0][:, e, cols], ident[:], is_transpose=True, start=False, stop=True)
            nc.scalar.copy(turned[:, j0 : j0 + 2], bank[:].rearrange("m j e p -> m j p e"))
        for c, width in enumerate(CHUNKS):
            bank = psum.tile([P, width], F32, name="back", tag="bank")
            for lo in range(0, width, P):
                words = turned[:, (starts[c] + lo) // P].rearrange("m p e -> m (p e)").bitcast(F32)
                nc.tensor.transpose(bank[:, lo : lo + P], words, ident[:])
            nc.scalar.copy(pairs[c][:, 0].rearrange("p m e -> p (m e)").bitcast(F32), bank[:])
        w_codes = kept([P, 2 * N], U32, "w_codes")
        w_scale = kept([P, 2 * N], U8, "w_scale")
        w_flat = w_bf[:].rearrange("p i n t -> p (i n t)")
        for lo, hi in ((0, 512), (512, 2 * N)):
            nc.vector.quantize_mx(out=w_codes[:, lo:hi].bitcast(FP8X4), scales=w_scale[:, lo:hi], in_=w_flat[:, PACK * lo : PACK * hi])
        put(3, 0, S)

        out_rows = out.rearrange("(b p) m -> p b m", p=P)
        x23 = {}
        z_bf = {}
        z_q = {}
        parts = {}

        def pick_chunk(c):
            x23[c] = kept([P, 2, CHUNKS[c]], F32, "x23_%d" % c, after="z_bf%d" % (c - 2) if c >= 2 else None)
            for e in range(2):
                pick(x23[c][:, e, :], 2 + e, starts[c], starts[c] + CHUNKS[c])

        def weave(c):
            add_flex(c, 1, x23[c][:])
            z_bf[c] = kept([P, CHUNKS[c], 2], F32, "z_bf%d" % c)
            nc.scalar.copy(
                z_bf[c][:], pairs[c][:].rearrange("p u m e -> p (u m e)").bitcast(F32).rearrange("p (u m) -> p m u", u=2)
            )

        def quantize(c):
            codes = ring.tile([P, CHUNKS[c]], U32, name="z_codes", align_bytes=64)
            scale = ring.tile([P, CHUNKS[c]], U8, name="z_scale", align_bytes=64)
            nc.vector.quantize_mx(
                out=codes[:].bitcast(FP8X4), scales=scale[:], in_=z_bf[c][:].rearrange("p m u -> p (m u)").bitcast(BF16)
            )
            ya = ring.tile([P, NB, CHUNKS[c]], F32, name="ya", bufs=3)
            yc = ring.tile([P, NB, CHUNKS[c]], F32, name="yc", bufs=3)
            yb = []
            for lo in range(0, CHUNKS[c], SUB):
                banks = [
                    psum.tile([P, NB, SUB], F32, name="y_a", tag="quick", bufs=2),
                    psum.tile([P, NB, SUB], F32, name="y_b", tag="bank"),
                    psum.tile([P, NB, SUB], F32, name="y_c", tag="quick", bufs=2),
                ]
                for i in (0, 2, 1):
                    for b in range(NB):
                        if i < 2:
                            cols = slice(i * N + b * P, i * N + (b + 1) * P)
                            lhs, lhs_scale = w_codes[:, cols], w_scale[:, cols]
                        else:
                            lhs, lhs_scale = wc_w[:, b * P : (b + 1) * P], wc_s[:, b * P : (b + 1) * P]
                        nc.tensor.matmul_mx(
                            out=banks[i][:, b, :],
                            lhsT=lhs.bitcast(FP8X4),
                            lhsT_scale=lhs_scale,
                            rhs=codes[:, lo : lo + SUB].bitcast(FP8X4),
                            rhs_scale=scale[:, lo : lo + SUB],
                            start=True,
                            stop=True,
                        )
                nc.scalar.copy(ya[:, :, lo : lo + SUB], banks[0][:])
                nc.scalar.activation(yc[:, :, lo : lo + SUB], banks[2][:], ACT.Abs)
                yb.append(banks[1])
            parts[c] = (ya, yb, yc)

        best = {}

        def larger(c):
            ya, yb, yc = parts[c]
            best[c] = ring.tile([P, NB, CHUNKS[c]], F32, name="best")
            for i, lo in enumerate(range(0, CHUNKS[c], SUB)):
                nc.vector.tensor_tensor(best[c][:, :, lo : lo + SUB], yb[i][:], ya[:, :, lo : lo + SUB], ALU.max)

        def finish(c):
            width = SUB if c == len(CHUNKS) - 1 else CHUNKS[c]
            for lo in range(0, CHUNKS[c], width):
                res = ring.tile([P, NB, width], F32, name="res", bufs=3)
                nc.vector.tensor_tensor(res[:], best[c][:, :, lo : lo + width], parts[c][2][:, :, lo : lo + width], ALU.subtract)
                nc.sync.dma_start(out_rows[:, :, starts[c] + lo : starts[c] + lo + width], res[:])

        last = len(CHUNKS)
        pick_chunk(0)
        for step in range(last + 1):
            if step < last:
                weave(step)
            if step == 0:
                pick_chunk(1)
            if step >= 1:
                larger(step - 1)
            if step < last:
                quantize(step)
            if step >= 1:
                finish(step - 1)
            if step + 2 < last:
                pick_chunk(step + 2)
